import numpy as np
import ml_dtypes


def mxq(x, axis, fmt="e4m3"):
    dtype, down = {"e4m3": (ml_dtypes.float8_e4m3fn, 7), "e5m2": (ml_dtypes.float8_e5m2, 14)}[fmt]
    v = np.moveaxis(np.asarray(x, np.float32).astype(ml_dtypes.bfloat16).astype(np.float64), axis, -1)
    blocks = v.reshape(v.shape[:-1] + (-1, 32))
    amax = np.abs(blocks).max(-1, keepdims=True)
    byte = np.maximum(np.where(amax > 0, np.frexp(amax)[1] - 1 + 127, 0) - down, 1)
    scale = np.exp2(byte - 127.0)
    codes = (blocks / scale).astype(np.float32).astype(dtype).astype(np.float64)
    return np.moveaxis((codes * scale).reshape(v.shape), -1, axis)


WIDE = False


def mx_kscale(k):
    if not WIDE:
        return np.ones(k)
    levels = np.array([30, -30])
    if k % 512:
        return np.exp2(np.random.permutation(np.resize(levels, k // 32))).repeat(32)
    a = np.empty((k // 512, 16))
    for p in range(k // 512):
        a[p, :8] = np.random.permutation(np.resize(levels, 8))
        for g in range(8):
            far = levels[np.abs(levels - a[p, g]) >= 10]
            a[p, g + 8] = far[np.random.randint(len(far))]
    return np.exp2(a.ravel()).repeat(32)


def f64(x):
    return np.asarray(x).astype(np.float64)


def striped(idx):
    return np.tile(np.asarray(idx).reshape(-1, 16).T, (8, 1)).astype(np.uint16)


def unstriped(offs):
    return offs[:16].T.reshape(-1).astype(np.int64)


def striped8(idx):
    return np.asarray(idx).reshape(8, -1, 16).transpose(0, 2, 1).reshape(128, -1).astype(np.uint16)


def unstriped8(offs):
    return offs.reshape(8, 16, -1).transpose(0, 2, 1).reshape(8, -1).astype(np.int64)


def pick8(x, idx, run):
    r = np.arange(len(x))
    return x[r[:, None], idx[r % (8 * run) // run]]


E2M1 = np.array([0.0, 0.5, 1.0, 1.5, 2.0, 3.0, 4.0, 6.0, -0.0, -0.5, -1.0, -1.5, -2.0, -3.0, -4.0, -6.0])


def pack_weight(w, fmt):
    k, n = w.shape
    w = f64(np.asarray(w, np.float32).astype(ml_dtypes.bfloat16)).reshape(k // 32, 32, n)
    amax = np.abs(w).max(1)
    if fmt in ("e4m3", "e5m2"):
        byte = np.frexp(amax)[1] - 1 + 127 - (7 if fmt == "e4m3" else 14)
    else:
        mant, ex = np.frexp(amax / 6.0)
        byte = np.where(mant > 0.5, ex, ex - 1) + 127
    byte = np.clip(np.where(amax > 0, byte, 1), 1, 254)
    scaled = (w * np.exp2(127.0 - byte)[:, None, :]).reshape(k, n).astype(np.float32)
    by_word = np.ascontiguousarray(scaled.reshape(k // 512, 128, 4, n).transpose(0, 1, 3, 2))
    if fmt in ("e4m3", "e5m2"):
        words = by_word.astype(ml_dtypes.float8_e4m3fn if fmt == "e4m3" else ml_dtypes.float8_e5m2).view(np.uint8)
    else:
        c = by_word.astype(ml_dtypes.float4_e2m1fn).view(np.uint8) & 0xF
        words = (c[..., 0::2] | (c[..., 1::2] << 4)).reshape(k // 512, 128, 2 * n)
    return np.ascontiguousarray(words), np.ascontiguousarray(byte.astype(np.uint8).reshape(k // 512, 16, n))


def unpack_weight(words, scales, fmt):
    g, _, n = scales.shape
    words = np.ascontiguousarray(words).reshape(g, 128, n, -1)
    if fmt in ("e4m3", "e5m2"):
        vals = words.view(ml_dtypes.float8_e4m3fn if fmt == "e4m3" else ml_dtypes.float8_e5m2).astype(np.float64)
    else:
        nib = np.empty((g, 128, n, 4), np.uint8)
        nib[..., 0::2] = words & 0xF
        nib[..., 1::2] = words >> 4
        vals = E2M1[nib]
    vals = vals * np.repeat(np.exp2(scales.astype(np.float64) - 127.0), 8, axis=1)[..., None]
    return vals.transpose(0, 1, 3, 2).reshape(g * 512, n)


K, T, J, R, V, C, D, O, N, E = 512, 1024, 256, 512, 1024, 512, 512, 256, 256, 512


def setup_inputs():
    n = np.random.standard_normal
    idx = np.random.permutation(V)[:R]
    idx2 = np.random.permutation(T)[:J]
    idx3 = np.stack([np.random.permutation(C)[:J] for _ in range(8)])
    idx4 = np.stack([np.random.permutation(D)[:J] for _ in range(8)])
    idx5 = np.random.permutation(C)[:O]
    idx6 = np.random.permutation(D)[:O]
    idx7 = np.stack([np.random.permutation(E)[:O] for _ in range(8)])
    fk = mx_kscale(K)
    fr = mx_kscale(R)
    tr = np.ones(V)
    tr[idx] = fr
    xtp = pack_weight(n((K, T)) / fk[:, None], "e2m1")
    wtp = pack_weight(n((K, V)) * 1 / np.sqrt(K) * fk[:, None] * tr, "e4m3")
    w2p = pack_weight(n((K, R)) * 1 / np.sqrt(K) * fk[:, None] * fr, "e5m2")
    wbp = pack_weight(n((R, N)) * 1 / np.sqrt(R) / fr[:, None], "e2m1")
    return {
        "xt_words": xtp[0],
        "xt_scales": xtp[1],
        "wt_words": wtp[0],
        "wt_scales": wtp[1],
        "w2_words": w2p[0],
        "w2_scales": w2p[1],
        "sa": (np.random.uniform(0.5, 1.6, (R, 1))).astype(np.float32),
        "sb": (np.random.uniform(0.5, 1.6, (R, 1))).astype(np.float32),
        "wb_words": wbp[0],
        "wb_scales": wbp[1],
        "offs": striped(idx),
        "offs2": striped(idx2),
        "offs3": striped8(idx3),
        "offs4": striped8(idx4),
        "offs5": striped(idx5),
        "offs6": striped(idx6),
        "offs7": striped8(idx7),
    }


def reference(xt_words, xt_scales, wt_words, wt_scales, w2_words, w2_scales, sa, sb, wb_words, wb_scales, offs, offs2, offs3, offs4, offs5, offs6, offs7):
    idx = unstriped(offs)
    idx2 = unstriped(offs2)
    idx3 = unstriped8(offs3)
    idx4 = unstriped8(offs4)
    idx5 = unstriped(offs5)
    idx6 = unstriped(offs6)
    idx7 = unstriped8(offs7)
    xtu = unpack_weight(xt_words, xt_scales, "e2m1")
    wtu = unpack_weight(wt_words, wt_scales, "e4m3")
    w2u = unpack_weight(w2_words, w2_scales, "e5m2")
    wbu = unpack_weight(wb_words, wb_scales, "e2m1")
    wtidxg = wtu[:, idx]
    xtidx2g = xtu[:, idx2]
    a = wtidxg.T @ xtidx2g
    b = w2u.T @ xtidx2g
    pw = np.zeros((R, C))
    pw[np.arange(R)[:, None], idx3[np.arange(R) % 512 // 64]] = a
    pv = np.zeros((R, D))
    pv[np.arange(R)[:, None], idx4[np.arange(R) % 512 // 64]] = b
    hid = np.abs(pw[:, idx5] * f64(sa) - pv[:, idx6] * f64(sb))
    hidq = mxq(hid, 0, "e5m2")
    p = wbu.T @ hidq
    y = np.zeros((N, E))
    y[np.arange(N)[:, None], idx7[np.arange(N) % 128 // 16]] = p
    return y

@@ -1,0 +1,224 @@
+from contextlib import ExitStack
+
+import concourse.mybir as mybir
+
+K, T, J, R, V, C, D, O, N, E = 512, 1024, 256, 512, 1024, 512, 512, 256, 256, 512
+FLOPS = 2 * K * R * J * 2 + 2 * R * N * O
+
+F32 = mybir.dt.float32
+BF16 = mybir.dt.bfloat16
+I32 = mybir.dt.int32
+U32 = mybir.dt.uint32
+U16 = mybir.dt.uint16
+U8 = mybir.dt.uint8
+E4M3 = mybir.dt.float8_e4m3fn_x4
+E5M2 = mybir.dt.float8_e5m2_x4
+E2M1 = mybir.dt.float4_e2m1fn_x4
+COPY = mybir.ActivationFunctionType.Copy
+ALU = mybir.AluOpType
+
+P = 128
+PACK = 4
+HALF = 128
+LANES = 16
+
+
+def tile_list_twoownboards_storeleads_one_ownpage_kernel(
+    tc, xt_words, xt_scales, wt_words, wt_scales, w2_words, w2_scales, sa, sb, wb_words, wb_scales,
+    offs, offs2, offs3, offs4, offs5, offs6, offs7, out,
+):
+    nc = tc.nc
+
+    with ExitStack() as ctx:
+        lists = ctx.enter_context(tc.tile_pool(name="lists", bufs=1))
+        pool = ctx.enter_context(tc.tile_pool(name="work", bufs=1))
+        psum = ctx.enter_context(tc.psum_pool(name="psum", bufs=1))
+
+        def load_list(src, name):
+            dst = lists.tile([P, src.shape[1]], U16, name=name)
+            nc.sync.dma_start(dst[:], src)
+            return dst
+
+        def entries(lst, first, count):
+            return lst[:, first // LANES : (first + count) // LANES]
+
+        def zeroed_plane(width, name):
+            plane = pool.tile([P, width], U8, name=name, align_bytes=64)
+            nc.vector.memset(plane[:].bitcast(I32), 0)
+            return plane
+
+        def load_scale_rows(queue, plane, scales):
+            for q in range(4):
+                queue.dma_start(plane[32 * q : 32 * q + 4, :].bitcast(I32), scales[0, 4 * q : 4 * q + 4, :].bitcast(I32))
+
+        def board(engine, name, tag):
+            tile_ = pool.tile([P, C], F32, name=name, tag=tag, align_bytes=64)
+            engine.memset(tile_[:], 0.0)
+            return tile_
+
+        xt_plane = zeroed_plane(T, "xt_plane")
+        w2_plane = zeroed_plane(2 * R, "w2_plane")
+        list2 = load_list(offs2, "list2")
+        list4 = load_list(offs4, "list4")
+        xt_table = pool.tile([P, T], U16, name="xt_table", tag="xt_table", align_bytes=64)
+        nc.sync.dma_start(xt_table[:].bitcast(I32), xt_words[0].bitcast(I32))
+        load_scale_rows(nc.sync, xt_plane, xt_scales)
+        w2_raw = pool.tile([P, R], I32, name="w2_raw", tag="w2_raw", align_bytes=64)
+        nc.sync.dma_start(w2_raw[:], w2_words[0].rearrange("p c r -> p (c r)").bitcast(I32))
+        w2_rows = w2_scales[0].bitcast(I32).rearrange("(u v r) c -> v r u c", u=2, v=2)
+        w2_plane_words = w2_plane[:].bitcast(I32)
+        for v in range(2):
+            nc.sync.dma_start(w2_plane_words[32 * v : 32 * v + 4, :].rearrange("r (u c) -> r u c", u=2), w2_rows[v])
+
+        pv = [board(nc.vector, "pv%d" % t, "pv%d" % t) for t in range(2)]
+        wt_plane = zeroed_plane(V, "wt_plane")
+        wb_plane = zeroed_plane(N, "wb_plane")
+
+        list1 = load_list(offs, "list1")
+        wt_table = pool.tile([P, V], U32, name="wt_table", tag="wt_table", align_bytes=64)
+        nc.sync.dma_start(wt_table[:].bitcast(I32), wt_words[0].rearrange("p c r -> p (c r)").bitcast(I32))
+        load_scale_rows(nc.sync, wt_plane, wt_scales)
+        list6 = load_list(offs6, "list6")
+        sb_cols = pool.tile([P, PACK], F32, name="sb_cols")
+        nc.sync.dma_start(sb_cols[:], sb.rearrange("(p t) o -> p (t o)", t=PACK))
+        list3 = load_list(offs3, "list3")
+        list5 = load_list(offs5, "list5")
+        sa_cols = pool.tile([P, PACK], F32, name="sa_cols")
+        nc.sync.dma_start(sa_cols[:], sa.rearrange("(p t) o -> p (t o)", t=PACK))
+        wb_codes = pool.tile([P, 2 * N], U8, name="wb_codes", align_bytes=64)
+        nc.sync.dma_start(wb_codes[:].bitcast(I32), wb_words[0].bitcast(I32))
+        load_scale_rows(nc.sync, wb_plane, wb_scales)
+        list7 = load_list(offs7, "list7")
+
+        x_codes = pool.tile([P, J], U16, name="x_codes", align_bytes=64)
+        x_scales = pool.tile([P, J], U8, name="x_scales", align_bytes=64)
+        w2_codes = pool.tile([P, R], I32, name="w2_codes", align_bytes=64)
+        w2_dealt = pool.tile([P, R], U8, name="w2_dealt", align_bytes=64)
+
+        def deal(dst, src, t0, t1):
+            nc.vector.tensor_copy(
+                dst[:, t0 * P : t1 * P].rearrange("p (t q) -> p t q", q=P),
+                src[:, 0:R].rearrange("p (q t) -> p t q", t=PACK)[:, t0:t1, :],
+            )
+
+        def product(bank, codes, scales, fmt, t, first, count):
+            nc.tensor.matmul_mx(
+                out=bank,
+                lhsT=codes[:, t * P : (t + 1) * P].bitcast(fmt),
+                lhsT_scale=scales[:, t * P : (t + 1) * P],
+                rhs=x_codes[:, first : first + count].bitcast(E2M1),
+                rhs_scale=x_scales[:, first : first + count],
+                start=True,
+                stop=True,
+            )
+
+        def scatter(window, lst, first, count, values):
+            nc.scalar.activation(out=window[:].indirect(entries(lst, first, count)), in_=values, func=COPY)
+
+        def fetch(dst, window, lst, h, scale):
+            nc.scalar.activation(out=dst, in_=window[:].indirect(entries(lst, h * HALF, HALF)), func=COPY, scale=scale)
+
+        nc.vector.tensor_copy(x_codes[:], xt_table[:].indirect(list2[:]))
+        nc.vector.tensor_copy(x_scales[:], xt_plane[:].indirect(list2[:]))
+        deal(w2_codes, w2_raw, 0, PACK)
+        nc.vector.tensor_copy(w2_plane_words[64:128, 0 : R // 4], w2_plane_words[0:64, R // 4 : R // 2])
+        b_rows = []
+        for t0, t1 in ((0, 1), (1, 2), (2, 4)):
+            deal(w2_dealt, w2_plane, t0, t1)
+            bank = psum.tile([P, t1 - t0, J], F32, name="b_bank%d" % t0)
+            for t in range(t0, t1):
+                product(bank[:, t - t0, :], w2_codes, w2_dealt, E5M2, t, 0, J)
+            rows = pool.tile([P, t1 - t0, J], F32, name="b_rows%d" % t0, tag="b_rows%d" % t0, align_bytes=64)
+            if t0 == 0:
+                nc.scalar.activation(out=rows[:], in_=bank[:], func=COPY)
+            else:
+                nc.vector.tensor_copy(rows[:], bank[:])
+            b_rows.extend(rows[:, t - t0, :] for t in range(t0, t1))
+        for t in range(2):
+            scatter(pv[t], list4, 0, J, b_rows[t])
+
+        pv = pv + [board(nc.gpsimd, "pv%d" % (t + 2), tag) for t, tag in enumerate(("w2_plane", "b_rows0"))]
+        w_codes = pool.tile([P, R], U32, name="w_codes", align_bytes=64)
+        w_scales = pool.tile([P, R], U8, name="w_scales", align_bytes=64)
+        for h in range(2):
+            for dst, table in ((w_codes, wt_table), (w_scales, wt_plane)):
+                nc.vector.tensor_copy(
+                    dst[:].rearrange("p (t q) -> p q t", t=PACK)[:, h * 64 : (h + 1) * 64, :],
+                    table[:].indirect(entries(list1, h * 256, 256)),
+                )
+        a_rows = pool.tile([P, PACK, J], F32, name="a_rows", tag="a_rows", align_bytes=64)
+        for u in range(2):
+            bank = psum.tile([P, 2, J], F32, name="a_bank%d" % u)
+            for t in range(2):
+                product(bank[:, t, :], w_codes, w_scales, E4M3, 2 * u + t, 0, J)
+            nc.vector.tensor_copy(a_rows[:, 2 * u : 2 * u + 2, :], bank[:])
+
+        pw = [board(nc.gpsimd, "pw%d" % t, tag) for t, tag in enumerate(("b_rows1", "wt_table", "w_codes", "w_scales"))]
+
+        picked = [pool.tile([P, 2, PACK, HALF], F32, name="picked0", align_bytes=64)]
+        diff = [pool.tile([P, PACK, HALF], F32, name="diff%d" % h, align_bytes=64) for h in range(2)]
+
+        def fetch_a(h, t):
+            fetch(picked[h][:, 0, t, :], pw[t], list5, h, sa_cols[:, t : t + 1])
+
+        def fetch_b(h, t):
+            fetch(picked[h][:, 1, t, :], pv[t], list6, h, sb_cols[:, t : t + 1])
+
+        def subtract(h, t):
+            nc.vector.tensor_tensor(diff[h][:, t, :], picked[h][:, 0, t, :], picked[h][:, 1, t, :], ALU.subtract)
+
+        scatter(pv[2], list4, 0, J, b_rows[2])
+        fetch_b(0, 0)
+        fetch_b(0, 1)
+        scatter(pv[3], list4, 0, J, b_rows[3])
+        fetch_b(0, 2)
+        for t in range(PACK):
+            scatter(pw[t], list3, 0, J, a_rows[:, t, :])
+            if t == 0:
+                fetch_b(0, 3)
+            else:
+                fetch_a(0, t - 1)
+                subtract(0, t - 1)
+        fetch_a(0, 3)
+        subtract(0, 3)
+
+        page = [board(nc.gpsimd, "page%d" % m, tag) for m, tag in enumerate(("x_codes", "x_scales"))]
+
+        def second_stage(h):
+            hid = pool.tile([P, HALF * PACK], BF16, name="hid%d" % h, align_bytes=64)
+            woven = diff[h][:].rearrange("p t o -> p o t")
+            nc.vector.scalar_tensor_tensor(
+                hid[:].rearrange("p (o t) -> p o t", t=PACK), woven, -1.0, woven, ALU.mult, ALU.max
+            )
+            codes = pool.tile([P, HALF], U32, name="hid_codes%d" % h, align_bytes=64)
+            scales = pool.tile([P, HALF], U8, name="hid_scales%d" % h, align_bytes=64)
+            nc.vector.quantize_mx(out=codes[:].bitcast(E5M2), scales=scales[:], in_=hid[:])
+            results = []
+            for m in range(2):
+                bank = psum.tile([P, HALF], F32, name="p_bank%d%d" % (h, m), tag=("b_bank0", "b_bank1", "b_bank2", "a_bank0")[2 * h + m])
+                nc.tensor.matmul_mx(
+                    out=bank[:],
+                    lhsT=wb_codes[:, 2 * m * P : 2 * (m + 1) * P].bitcast(E2M1),
+                    lhsT_scale=wb_plane[:, m * P : (m + 1) * P],
+                    rhs=codes[:].bitcast(E5M2),
+                    rhs_scale=scales[:],
+                    start=True,
+                    stop=True,
+                )
+                rows = pool.tile([P, HALF], F32, name="p_rows%d%d" % (h, m), align_bytes=64)
+                nc.vector.tensor_copy(rows[:], bank[:])
+                results.append(rows)
+            return results
+
+        first = second_stage(0)
+        picked.append(pool.tile([P, 2, PACK, HALF], F32, name="picked1", tag="a_rows", align_bytes=64))
+        for t in range(PACK):
+            fetch_a(1, t)
+            fetch_b(1, t)
+            subtract(1, t)
+        for m in range(2):
+            scatter(page[m], list7, 0, HALF, first[m][:])
+        second = second_stage(1)
+        for m in range(2):
+            scatter(page[m], list7, HALF, HALF, second[m][:])
+            nc.sync.dma_start(out[m * P : (m + 1) * P, :], page[m][:])

@@ -32,6 +32,8 @@ def tile_list_twoownboards_storeleads_one_ownpage_kernel(
     with ExitStack() as ctx:
         lists = ctx.enter_context(tc.tile_pool(name="lists", bufs=1))
         pool = ctx.enter_context(tc.tile_pool(name="work", bufs=1))
+        reused = ctx.enter_context(tc.tile_pool(name="reused", bufs=1))
+        boards = ctx.enter_context(tc.tile_pool(name="boards", bufs=1))
         psum = ctx.enter_context(tc.psum_pool(name="psum", bufs=1))
 
         def load_list(src, name):
@@ -47,28 +49,33 @@ def tile_list_twoownboards_storeleads_one_ownpage_kernel(
             nc.vector.memset(plane[:].bitcast(I32), 0)
             return plane
 
-        def load_scale_rows(queue, plane, scales):
-            for q in range(4):
+        def load_scale_rows(queue, plane, scales, quadrants=range(4)):
+            for q in quadrants:
                 queue.dma_start(plane[32 * q : 32 * q + 4, :].bitcast(I32), scales[0, 4 * q : 4 * q + 4, :].bitcast(I32))
 
-        def board(engine, name, tag):
-            tile_ = pool.tile([P, C], F32, name=name, tag=tag, align_bytes=64)
+        def board(engine, name, tag, offset=None):
+            if offset is None:
+                tile_ = pool.tile([P, C], F32, name=name, tag=tag, align_bytes=64)
+            else:
+                tile_ = boards.tile([P, C], F32, name=name, offset=offset, align_bytes=64)
             engine.memset(tile_[:], 0.0)
             return tile_
 
-        xt_plane = zeroed_plane(T, "xt_plane")
         w2_plane = zeroed_plane(2 * R, "w2_plane")
+        xt_plane = reused.tile([P, T], U8, name="xt_plane", offset=0, align_bytes=64)
+        nc.vector.memset(xt_plane[:].bitcast(I32), 0)
         list2 = load_list(offs2, "list2")
-        list4 = load_list(offs4, "list4")
         xt_table = pool.tile([P, T], U16, name="xt_table", tag="xt_table", align_bytes=64)
         nc.sync.dma_start(xt_table[:].bitcast(I32), xt_words[0].bitcast(I32))
-        load_scale_rows(nc.sync, xt_plane, xt_scales)
-        w2_raw = pool.tile([P, R], I32, name="w2_raw", tag="w2_raw", align_bytes=64)
-        nc.sync.dma_start(w2_raw[:], w2_words[0].rearrange("p c r -> p (c r)").bitcast(I32))
         w2_rows = w2_scales[0].bitcast(I32).rearrange("(u v r) c -> v r u c", u=2, v=2)
         w2_plane_words = w2_plane[:].bitcast(I32)
         for v in range(2):
             nc.sync.dma_start(w2_plane_words[32 * v : 32 * v + 4, :].rearrange("r (u c) -> r u c", u=2), w2_rows[v])
+        load_scale_rows(nc.sync, xt_plane, xt_scales, range(0, 3))
+        w2_raw = pool.tile([P, R], I32, name="w2_raw", tag="w2_raw", align_bytes=64)
+        nc.sync.dma_start(w2_raw[:], w2_words[0].rearrange("p c r -> p (c r)").bitcast(I32))
+        load_scale_rows(nc.sync, xt_plane, xt_scales, range(3, 4))
+        list4 = load_list(offs4, "list4")
 
         pv = [board(nc.vector, "pv%d" % t, "pv%d" % t) for t in range(2)]
         wt_plane = zeroed_plane(V, "wt_plane")
@@ -90,24 +97,19 @@ def tile_list_twoownboards_storeleads_one_ownpage_kernel(
         load_scale_rows(nc.sync, wb_plane, wb_scales)
         list7 = load_list(offs7, "list7")
 
-        x_codes = pool.tile([P, J], U16, name="x_codes", align_bytes=64)
-        x_scales = pool.tile([P, J], U8, name="x_scales", align_bytes=64)
-        w2_codes = pool.tile([P, R], I32, name="w2_codes", align_bytes=64)
-        w2_dealt = pool.tile([P, R], U8, name="w2_dealt", align_bytes=64)
-
-        def deal(dst, src, t0, t1):
+        def deal(dst, src, t0):
             nc.vector.tensor_copy(
-                dst[:, t0 * P : t1 * P].rearrange("p (t q) -> p t q", q=P),
-                src[:, 0:R].rearrange("p (q t) -> p t q", t=PACK)[:, t0:t1, :],
+                dst[:].rearrange("p (t q) -> p t q", q=P),
+                src[:, 0:R].rearrange("p (q t) -> p t q", t=PACK)[:, t0 : t0 + 2, :],
             )
 
-        def product(bank, codes, scales, fmt, t, first, count):
+        def product(bank, codes, scales, fmt, t, h):
             nc.tensor.matmul_mx(
                 out=bank,
                 lhsT=codes[:, t * P : (t + 1) * P].bitcast(fmt),
                 lhsT_scale=scales[:, t * P : (t + 1) * P],
-                rhs=x_codes[:, first : first + count].bitcast(E2M1),
-                rhs_scale=x_scales[:, first : first + count],
+                rhs=x_codes[h][:].bitcast(E2M1),
+                rhs_scale=x_scales[h][:],
                 start=True,
                 stop=True,
             )
@@ -118,30 +120,55 @@ def tile_list_twoownboards_storeleads_one_ownpage_kernel(
         def fetch(dst, window, lst, h, scale):
             nc.scalar.activation(out=dst, in_=window[:].indirect(entries(lst, h * HALF, HALF)), func=COPY, scale=scale)
 
-        nc.vector.tensor_copy(x_codes[:], xt_table[:].indirect(list2[:]))
-        nc.vector.tensor_copy(x_scales[:], xt_plane[:].indirect(list2[:]))
-        deal(w2_codes, w2_raw, 0, PACK)
+        x_codes = [pool.tile([P, HALF], U16, name="x_codes0", align_bytes=64)]
+        x_scales = [pool.tile([P, HALF], U8, name="x_scales%d" % h, align_bytes=64) for h in range(2)]
+        w2_codes = [pool.tile([P, 2 * P], I32, name="w2_codes0", align_bytes=64)]
+        w2_dealt = [pool.tile([P, 2 * P], U8, name="w2_dealt0", align_bytes=64)]
+        nc.vector.tensor_copy(x_codes[0][:], xt_table[:].indirect(entries(list2, 0, HALF)))
         nc.vector.tensor_copy(w2_plane_words[64:128, 0 : R // 4], w2_plane_words[0:64, R // 4 : R // 2])
-        b_rows = []
-        for t0, t1 in ((0, 1), (1, 2), (2, 4)):
-            deal(w2_dealt, w2_plane, t0, t1)
-            bank = psum.tile([P, t1 - t0, J], F32, name="b_bank%d" % t0)
-            for t in range(t0, t1):
-                product(bank[:, t - t0, :], w2_codes, w2_dealt, E5M2, t, 0, J)
-            rows = pool.tile([P, t1 - t0, J], F32, name="b_rows%d" % t0, tag="b_rows%d" % t0, align_bytes=64)
-            if t0 == 0:
+        deal(w2_dealt[0], w2_plane, 0)
+        deal(w2_codes[0], w2_raw, 0)
+        for h in range(2):
+            nc.vector.tensor_copy(x_scales[h][:], xt_plane[:].indirect(entries(list2, h * HALF, HALF)))
+        x_codes.append(reused.tile([P, HALF], U16, name="x_codes1", offset=0, align_bytes=64))
+        nc.vector.tensor_copy(x_codes[1][:], xt_table[:].indirect(entries(list2, HALF, HALF)))
+
+        for t in range(2):
+            bank = psum.tile([P, HALF], F32, name="b_first%d" % t)
+            product(bank[:], w2_codes[0], w2_dealt[0], E5M2, t, 0)
+            rows = pool.tile([P, HALF], F32, name="b_lead%d" % t, align_bytes=64)
+            if t == 0:
                 nc.scalar.activation(out=rows[:], in_=bank[:], func=COPY)
             else:
                 nc.vector.tensor_copy(rows[:], bank[:])
-            b_rows.extend(rows[:, t - t0, :] for t in range(t0, t1))
+            scatter(pv[t], list4, 0, HALF, rows[:])
+        bank = psum.tile([P, 2, HALF], F32, name="b_bank1")
         for t in range(2):
-            scatter(pv[t], list4, 0, J, b_rows[t])
+            product(bank[:, t, :], w2_codes[0], w2_dealt[0], E5M2, t, 1)
+        rows = pool.tile([P, 2, HALF], F32, name="b_rows1", align_bytes=64)
+        nc.vector.tensor_copy(rows[:], bank[:])
+        for t in range(2):
+            scatter(pv[t], list4, HALF, HALF, rows[:, t, :])
 
-        pv = pv + [board(nc.gpsimd, "pv%d" % (t + 2), tag) for t, tag in enumerate(("w2_plane", "b_rows0"))]
+        w2_dealt.append(reused.tile([P, 2 * P], U8, name="w2_dealt1", offset=256, align_bytes=64))
+        w2_codes.append(reused.tile([P, 2 * P], I32, name="w2_codes1", offset=512, align_bytes=64))
+        deal(w2_dealt[1], w2_plane, 2)
+        deal(w2_codes[1], w2_raw, 2)
+        bank = psum.tile([P, 2, J], F32, name="b_bank2")
+        for t in range(2):
+            for h in range(2):
+                product(bank[:, t, h * HALF : (h + 1) * HALF], w2_codes[1], w2_dealt[1], E5M2, t, h)
+        b_rest = []
+        for t in range(2):
+            rows = boards.tile([P, J], F32, name="b_rest%d" % t, offset=4096 * t + 1536, align_bytes=64)
+            nc.vector.tensor_copy(rows[:], bank[:, t, :])
+            b_rest.append(rows)
+
+        pv = pv + [board(nc.gpsimd, "pv%d" % (t + 2), tag) for t, tag in enumerate(("b_lead1", "b_rows1"))]
         w_codes = pool.tile([P, R], U32, name="w_codes", align_bytes=64)
-        w_scales = pool.tile([P, R], U8, name="w_scales", align_bytes=64)
-        for h in range(2):
-            for dst, table in ((w_codes, wt_table), (w_scales, wt_plane)):
+        w_scales = reused.tile([P, R], U8, name="w_scales", offset=512, align_bytes=64)
+        for dst, table in ((w_codes, wt_table), (w_scales, wt_plane)):
+            for h in range(2):
                 nc.vector.tensor_copy(
                     dst[:].rearrange("p (t q) -> p q t", t=PACK)[:, h * 64 : (h + 1) * 64, :],
                     table[:].indirect(entries(list1, h * 256, 256)),
@@ -150,10 +177,10 @@ def tile_list_twoownboards_storeleads_one_ownpage_kernel(
         for u in range(2):
             bank = psum.tile([P, 2, J], F32, name="a_bank%d" % u)
             for t in range(2):
-                product(bank[:, t, :], w_codes, w_scales, E4M3, 2 * u + t, 0, J)
+                for h in range(2):
+                    product(bank[:, t, h * HALF : (h + 1) * HALF], w_codes, w_scales, E4M3, 2 * u + t, h)
             nc.vector.tensor_copy(a_rows[:, 2 * u : 2 * u + 2, :], bank[:])
 
-        pw = [board(nc.gpsimd, "pw%d" % t, tag) for t, tag in enumerate(("b_rows1", "wt_table", "w_codes", "w_scales"))]
 
         picked = [pool.tile([P, 2, PACK, HALF], F32, name="picked0", align_bytes=64)]
         diff = [pool.tile([P, PACK, HALF], F32, name="diff%d" % h, align_bytes=64) for h in range(2)]
@@ -167,10 +194,11 @@ def tile_list_twoownboards_storeleads_one_ownpage_kernel(
         def subtract(h, t):
             nc.vector.tensor_tensor(diff[h][:, t, :], picked[h][:, 0, t, :], picked[h][:, 1, t, :], ALU.subtract)
 
-        scatter(pv[2], list4, 0, J, b_rows[2])
+        scatter(pv[2], list4, 0, J, b_rest[0][:])
         fetch_b(0, 0)
         fetch_b(0, 1)
-        scatter(pv[3], list4, 0, J, b_rows[3])
+        scatter(pv[3], list4, 0, J, b_rest[1][:])
+        pw = [board(nc.gpsimd, "pw%d" % t, None, 2048 * t) for t in range(PACK)]
         fetch_b(0, 2)
         for t in range(PACK):
             scatter(pw[t], list3, 0, J, a_rows[:, t, :])
@@ -182,7 +210,7 @@ def tile_list_twoownboards_storeleads_one_ownpage_kernel(
         fetch_a(0, 3)
         subtract(0, 3)
 
-        page = [board(nc.gpsimd, "page%d" % m, tag) for m, tag in enumerate(("x_codes", "x_scales"))]
+        page = [board(nc.gpsimd, "page%d" % m, tag) for m, tag in enumerate(("x_codes0", "x_scales0"))]
 
         def second_stage(h):
             hid = pool.tile([P, HALF * PACK], BF16, name="hid%d" % h, align_bytes=64)
@@ -193,11 +221,12 @@ def tile_list_twoownboards_storeleads_one_ownpage_kernel(
             codes = pool.tile([P, HALF], U32, name="hid_codes%d" % h, align_bytes=64)
             scales = pool.tile([P, HALF], U8, name="hid_scales%d" % h, align_bytes=64)
             nc.vector.quantize_mx(out=codes[:].bitcast(E5M2), scales=scales[:], in_=hid[:])
-            results = []
+            rows = pool.tile([P, 2, HALF], F32, name="p_rows%d" % h, align_bytes=64)
             for m in range(2):
-                bank = psum.tile([P, HALF], F32, name="p_bank%d%d" % (h, m), tag=("b_bank0", "b_bank1", "b_bank2", "a_bank0")[2 * h + m])
+                if h == 1 or m == 0:
+                    bank = psum.tile([P, 2, HALF], F32, name="p_bank%d%d" % (h, m), tag=("b_first0", "b_bank1", "b_bank2")[h + m])
                 nc.tensor.matmul_mx(
-                    out=bank[:],
+                    out=bank[:, m, :],
                     lhsT=wb_codes[:, 2 * m * P : 2 * (m + 1) * P].bitcast(E2M1),
                     lhsT_scale=wb_plane[:, m * P : (m + 1) * P],
                     rhs=codes[:].bitcast(E5M2),
@@ -205,20 +234,20 @@ def tile_list_twoownboards_storeleads_one_ownpage_kernel(
                     start=True,
                     stop=True,
                 )
-                rows = pool.tile([P, HALF], F32, name="p_rows%d%d" % (h, m), align_bytes=64)
-                nc.vector.tensor_copy(rows[:], bank[:])
-                results.append(rows)
-            return results
+                if h == 1:
+                    nc.vector.tensor_copy(rows[:, m, :], bank[:, m, :])
+            return rows, bank
 
-        first = second_stage(0)
+        first, first_bank = second_stage(0)
         picked.append(pool.tile([P, 2, PACK, HALF], F32, name="picked1", tag="a_rows", align_bytes=64))
         for t in range(PACK):
             fetch_a(1, t)
             fetch_b(1, t)
             subtract(1, t)
+        nc.scalar.activation(out=first[:], in_=first_bank[:], func=COPY)
         for m in range(2):
-            scatter(page[m], list7, 0, HALF, first[m][:])
-        second = second_stage(1)
+            scatter(page[m], list7, 0, HALF, first[:, m, :])
+        second, last_bank = second_stage(1)
         for m in range(2):
-            scatter(page[m], list7, HALF, HALF, second[m][:])
+            scatter(page[m], list7, HALF, HALF, second[:, m, :])
             nc.sync.dma_start(out[m * P : (m + 1) * P, :], page[m][:])

@@ -34,6 +34,7 @@ def tile_list_twoownboards_storeleads_one_ownpage_kernel(
         pool = ctx.enter_context(tc.tile_pool(name="work", bufs=1))
         reused = ctx.enter_context(tc.tile_pool(name="reused", bufs=1))
         boards = ctx.enter_context(tc.tile_pool(name="boards", bufs=1))
+        late = ctx.enter_context(tc.tile_pool(name="late", bufs=1))
         psum = ctx.enter_context(tc.psum_pool(name="psum", bufs=1))
 
         def load_list(src, name):
@@ -60,6 +61,10 @@ def tile_list_twoownboards_storeleads_one_ownpage_kernel(
                 tile_ = boards.tile([P, C], F32, name=name, offset=offset, align_bytes=64)
             engine.memset(tile_[:], 0.0)
             return tile_
+
+        def whole_bank(name, rows, width, tag=None):
+            bank = psum.tile([P, 512], F32, name=name, tag=tag or name)
+            return bank[:, 0 : rows * width].rearrange("p (r w) -> p r w", r=rows)
 
         w2_plane = zeroed_plane(2 * R, "w2_plane")
         xt_plane = reused.tile([P, T], U8, name="xt_plane", offset=0, align_bytes=64)
@@ -117,8 +122,8 @@ def tile_list_twoownboards_storeleads_one_ownpage_kernel(
         def scatter(window, lst, first, count, values):
             nc.scalar.activation(out=window[:].indirect(entries(lst, first, count)), in_=values, func=COPY)
 
-        def fetch(dst, window, lst, h, scale):
-            nc.scalar.activation(out=dst, in_=window[:].indirect(entries(lst, h * HALF, HALF)), func=COPY, scale=scale)
+        def fetch(dst, window, lst, first, count, scale):
+            nc.scalar.activation(out=dst, in_=window[:].indirect(entries(lst, first, count)), func=COPY, scale=scale)
 
         x_codes = [pool.tile([P, HALF], U16, name="x_codes0", align_bytes=64)]
         x_scales = [pool.tile([P, HALF], U8, name="x_scales%d" % h, align_bytes=64) for h in range(2)]
@@ -134,19 +139,19 @@ def tile_list_twoownboards_storeleads_one_ownpage_kernel(
         nc.vector.tensor_copy(x_codes[1][:], xt_table[:].indirect(entries(list2, HALF, HALF)))
 
         for t in range(2):
-            bank = psum.tile([P, HALF], F32, name="b_first%d" % t)
-            product(bank[:], w2_codes[0], w2_dealt[0], E5M2, t, 0)
-            rows = pool.tile([P, HALF], F32, name="b_lead%d" % t, align_bytes=64)
+            bank = whole_bank("b_first%d" % t, 1, HALF)[:, 0, :]
+            product(bank, w2_codes[0], w2_dealt[0], E5M2, t, 0)
+            rows = pool.tile([P, HALF], F32, name="b_lead%d" % t, tag=("b_lead0", "xt_table")[t], align_bytes=64)
             if t == 0:
-                nc.scalar.activation(out=rows[:], in_=bank[:], func=COPY)
+                nc.scalar.activation(out=rows[:], in_=bank, func=COPY)
             else:
-                nc.vector.tensor_copy(rows[:], bank[:])
+                nc.vector.tensor_copy(rows[:], bank)
             scatter(pv[t], list4, 0, HALF, rows[:])
-        bank = psum.tile([P, 2, HALF], F32, name="b_bank1")
+        bank = whole_bank("b_bank1", 2, HALF)
         for t in range(2):
             product(bank[:, t, :], w2_codes[0], w2_dealt[0], E5M2, t, 1)
         rows = pool.tile([P, 2, HALF], F32, name="b_rows1", align_bytes=64)
-        nc.vector.tensor_copy(rows[:], bank[:])
+        nc.vector.tensor_copy(rows[:], bank)
         for t in range(2):
             scatter(pv[t], list4, HALF, HALF, rows[:, t, :])
 
@@ -164,35 +169,36 @@ def tile_list_twoownboards_storeleads_one_ownpage_kernel(
             nc.vector.tensor_copy(rows[:], bank[:, t, :])
             b_rest.append(rows)
 
-        pv = pv + [board(nc.gpsimd, "pv%d" % (t + 2), tag) for t, tag in enumerate(("b_lead1", "b_rows1"))]
-        w_codes = pool.tile([P, R], U32, name="w_codes", align_bytes=64)
-        w_scales = reused.tile([P, R], U8, name="w_scales", offset=512, align_bytes=64)
-        for dst, table in ((w_codes, wt_table), (w_scales, wt_plane)):
-            for h in range(2):
-                nc.vector.tensor_copy(
-                    dst[:].rearrange("p (t q) -> p q t", t=PACK)[:, h * 64 : (h + 1) * 64, :],
-                    table[:].indirect(entries(list1, h * 256, 256)),
-                )
-        a_rows = pool.tile([P, PACK, J], F32, name="a_rows", tag="a_rows", align_bytes=64)
+        pv = pv + [board(nc.gpsimd, "pv%d" % (t + 2), tag) for t, tag in enumerate(("xt_table", "b_rows1"))]
+        w_picked = pool.tile([P, R], U32, name="w_picked", align_bytes=64)
+        w_picked_scales = reused.tile([P, R], U8, name="w_picked_scales", offset=512, align_bytes=64)
+        nc.vector.tensor_copy(w_picked[:], wt_table[:].indirect(list1[:]))
+        nc.vector.tensor_copy(w_picked_scales[:], wt_plane[:].indirect(list1[:]))
+        a_rows = late.tile([P, PACK, J], F32, name="a_rows", offset=0, align_bytes=64)
         for u in range(2):
+            w_codes = pool.tile([P, 2 * P], U32, name="w_codes%d" % u, align_bytes=64)
+            w_scales = pool.tile([P, 2 * P], U8, name="w_scales%d" % u, align_bytes=64)
+            deal(w_codes, w_picked, 2 * u)
+            deal(w_scales, w_picked_scales, 2 * u)
             bank = psum.tile([P, 2, J], F32, name="a_bank%d" % u)
             for t in range(2):
                 for h in range(2):
-                    product(bank[:, t, h * HALF : (h + 1) * HALF], w_codes, w_scales, E4M3, 2 * u + t, h)
+                    product(bank[:, t, h * HALF : (h + 1) * HALF], w_codes, w_scales, E4M3, t, h)
             nc.vector.tensor_copy(a_rows[:, 2 * u : 2 * u + 2, :], bank[:])
-
 
         picked = [pool.tile([P, 2, PACK, HALF], F32, name="picked0", align_bytes=64)]
         diff = [pool.tile([P, PACK, HALF], F32, name="diff%d" % h, align_bytes=64) for h in range(2)]
 
-        def fetch_a(h, t):
-            fetch(picked[h][:, 0, t, :], pw[t], list5, h, sa_cols[:, t : t + 1])
+        def fetch_a(h, t, lo=0, hi=HALF):
+            fetch(picked[h][:, 0, t, lo:hi], pw[t], list5, h * HALF + lo, hi - lo, sa_cols[:, t : t + 1])
 
-        def fetch_b(h, t):
-            fetch(picked[h][:, 1, t, :], pv[t], list6, h, sb_cols[:, t : t + 1])
+        def fetch_b(h, t, lo=0, hi=HALF):
+            fetch(picked[h][:, 1, t, lo:hi], pv[t], list6, h * HALF + lo, hi - lo, sb_cols[:, t : t + 1])
 
-        def subtract(h, t):
-            nc.vector.tensor_tensor(diff[h][:, t, :], picked[h][:, 0, t, :], picked[h][:, 1, t, :], ALU.subtract)
+        def subtract(h, t, lo=0, hi=HALF):
+            nc.vector.tensor_tensor(
+                diff[h][:, t, lo:hi], picked[h][:, 0, t, lo:hi], picked[h][:, 1, t, lo:hi], ALU.subtract
+            )
 
         scatter(pv[2], list4, 0, J, b_rest[0][:])
         fetch_b(0, 0)
@@ -207,47 +213,61 @@ def tile_list_twoownboards_storeleads_one_ownpage_kernel(
             else:
                 fetch_a(0, t - 1)
                 subtract(0, t - 1)
-        fetch_a(0, 3)
-        subtract(0, 3)
+        for lo in (0, HALF // 2):
+            fetch_a(0, PACK - 1, lo, lo + HALF // 2)
+            subtract(0, PACK - 1, lo, lo + HALF // 2)
 
         page = [board(nc.gpsimd, "page%d" % m, tag) for m, tag in enumerate(("x_codes0", "x_scales0"))]
 
-        def second_stage(h):
-            hid = pool.tile([P, HALF * PACK], BF16, name="hid%d" % h, align_bytes=64)
-            woven = diff[h][:].rearrange("p t o -> p o t")
-            nc.vector.scalar_tensor_tensor(
-                hid[:].rearrange("p (o t) -> p o t", t=PACK), woven, -1.0, woven, ALU.mult, ALU.max
-            )
-            codes = pool.tile([P, HALF], U32, name="hid_codes%d" % h, align_bytes=64)
-            scales = pool.tile([P, HALF], U8, name="hid_scales%d" % h, align_bytes=64)
-            nc.vector.quantize_mx(out=codes[:].bitcast(E5M2), scales=scales[:], in_=hid[:])
-            rows = pool.tile([P, 2, HALF], F32, name="p_rows%d" % h, align_bytes=64)
-            for m in range(2):
-                if h == 1 or m == 0:
-                    bank = psum.tile([P, 2, HALF], F32, name="p_bank%d%d" % (h, m), tag=("b_first0", "b_bank1", "b_bank2")[h + m])
-                nc.tensor.matmul_mx(
-                    out=bank[:, m, :],
-                    lhsT=wb_codes[:, 2 * m * P : 2 * (m + 1) * P].bitcast(E2M1),
-                    lhsT_scale=wb_plane[:, m * P : (m + 1) * P],
-                    rhs=codes[:].bitcast(E5M2),
-                    rhs_scale=scales[:],
-                    start=True,
-                    stop=True,
-                )
-                if h == 1:
-                    nc.vector.tensor_copy(rows[:, m, :], bank[:, m, :])
-            return rows, bank
+        hid = [pool.tile([P, HALF * PACK], BF16, name="hid%d" % h, align_bytes=64) for h in range(2)]
+        hid_codes = [pool.tile([P, HALF], U32, name="hid_codes%d" % h, align_bytes=64) for h in range(2)]
+        hid_scales = [pool.tile([P, HALF], U8, name="hid_scales%d" % h, align_bytes=64) for h in range(2)]
 
-        first, first_bank = second_stage(0)
-        picked.append(pool.tile([P, 2, PACK, HALF], F32, name="picked1", tag="a_rows", align_bytes=64))
-        for t in range(PACK):
+        def quantise(h, lo=0, hi=HALF):
+            values = hid[h][:, lo * PACK : hi * PACK]
+            woven = diff[h][:, :, lo:hi].rearrange("p t o -> p o t")
+            nc.vector.scalar_tensor_tensor(
+                values.rearrange("p (o t) -> p o t", t=PACK), woven, -1.0, woven, ALU.mult, ALU.max
+            )
+            nc.vector.quantize_mx(out=hid_codes[h][:, lo:hi].bitcast(E5M2), scales=hid_scales[h][:, lo:hi], in_=values)
+
+        def output_product(bank, h, m):
+            nc.tensor.matmul_mx(
+                out=bank,
+                lhsT=wb_codes[:, 2 * m * P : 2 * (m + 1) * P].bitcast(E2M1),
+                lhsT_scale=wb_plane[:, m * P : (m + 1) * P],
+                rhs=hid_codes[h][:].bitcast(E5M2),
+                rhs_scale=hid_scales[h][:],
+                start=True,
+                stop=True,
+            )
+
+        for lo in (0, HALF // 2):
+            quantise(0, lo, lo + HALF // 2)
+        banks = [whole_bank("p_bank0%d" % m, 1, HALF, ("b_first0", "a_bank0")[m])[:, 0, :] for m in range(2)]
+        for m in range(2):
+            output_product(banks[m], 0, m)
+        picked.append(late.tile([P, 2, PACK, HALF], F32, name="picked1", offset=0, align_bytes=64))
+        for t in range(PACK - 1):
             fetch_a(1, t)
             fetch_b(1, t)
             subtract(1, t)
-        nc.scalar.activation(out=first[:], in_=first_bank[:], func=COPY)
+        for lo in (0, HALF // 2):
+            fetch_a(1, PACK - 1, lo, lo + HALF // 2)
+            fetch_b(1, PACK - 1, lo, lo + HALF // 2)
+            subtract(1, PACK - 1, lo, lo + HALF // 2)
+            quantise(1, lo, lo + HALF // 2)
         for m in range(2):
-            scatter(page[m], list7, 0, HALF, first[:, m, :])
-        second, last_bank = second_stage(1)
+            rows = pool.tile([P, HALF], F32, name="p_rows0%d" % m, align_bytes=64)
+            if m == 0:
+                nc.scalar.activation(out=rows[:], in_=banks[m], func=COPY)
+            else:
+                nc.vector.tensor_copy(rows[:], banks[m])
+            scatter(page[m], list7, 0, HALF, rows[:])
         for m in range(2):
-            scatter(page[m], list7, HALF, HALF, second[:, m, :])
+            bank = whole_bank("p_bank1%d" % m, 1, HALF, ("b_first1", "b_bank1")[m])[:, 0, :]
+            output_product(bank, 1, m)
+            rows = pool.tile([P, HALF], F32, name="p_rows1%d" % m, align_bytes=64)
+            nc.vector.tensor_copy(rows[:], bank)
+            scatter(page[m], list7, HALF, HALF, rows[:])
             nc.sync.dma_start(out[m * P : (m + 1) * P, :], page[m][:])

@@ -141,11 +141,8 @@ def tile_list_twoownboards_storeleads_one_ownpage_kernel(
         for t in range(2):
             bank = whole_bank("b_first%d" % t, 1, HALF)[:, 0, :]
             product(bank, w2_codes[0], w2_dealt[0], E5M2, t, 0)
-            rows = pool.tile([P, HALF], F32, name="b_lead%d" % t, tag=("b_lead0", "xt_table")[t], align_bytes=64)
-            if t == 0:
-                nc.scalar.activation(out=rows[:], in_=bank, func=COPY)
-            else:
-                nc.vector.tensor_copy(rows[:], bank)
+            rows = pool.tile([P, HALF], F32, name="b_lead%d" % t, align_bytes=64)
+            nc.scalar.activation(out=rows[:], in_=bank, func=COPY)
             scatter(pv[t], list4, 0, HALF, rows[:])
         bank = whole_bank("b_bank1", 2, HALF)
         for t in range(2):
@@ -169,7 +166,7 @@ def tile_list_twoownboards_storeleads_one_ownpage_kernel(
             nc.vector.tensor_copy(rows[:], bank[:, t, :])
             b_rest.append(rows)
 
-        pv = pv + [board(nc.gpsimd, "pv%d" % (t + 2), tag) for t, tag in enumerate(("xt_table", "b_rows1"))]
+        pv = pv + [board(nc.gpsimd, "pv%d" % (t + 2), tag) for t, tag in enumerate(("b_lead1", "b_rows1"))]
         w_picked = pool.tile([P, R], U32, name="w_picked", align_bytes=64)
         w_picked_scales = reused.tile([P, R], U8, name="w_picked_scales", offset=512, align_bytes=64)
         nc.vector.tensor_copy(w_picked[:], wt_table[:].indirect(list1[:]))

@@ -33,7 +33,6 @@ def tile_list_twoownboards_storeleads_one_ownpage_kernel(
         lists = ctx.enter_context(tc.tile_pool(name="lists", bufs=1))
         pool = ctx.enter_context(tc.tile_pool(name="work", bufs=1))
         reused = ctx.enter_context(tc.tile_pool(name="reused", bufs=1))
-        boards = ctx.enter_context(tc.tile_pool(name="boards", bufs=1))
         late = ctx.enter_context(tc.tile_pool(name="late", bufs=1))
         psum = ctx.enter_context(tc.psum_pool(name="psum", bufs=1))
 
@@ -54,11 +53,8 @@ def tile_list_twoownboards_storeleads_one_ownpage_kernel(
             for q in quadrants:
                 queue.dma_start(plane[32 * q : 32 * q + 4, :].bitcast(I32), scales[0, 4 * q : 4 * q + 4, :].bitcast(I32))
 
-        def board(engine, name, tag, offset=None):
-            if offset is None:
-                tile_ = pool.tile([P, C], F32, name=name, tag=tag, align_bytes=64)
-            else:
-                tile_ = boards.tile([P, C], F32, name=name, offset=offset, align_bytes=64)
+        def board(engine, name, tag):
+            tile_ = pool.tile([P, C], F32, name=name, tag=tag, align_bytes=64)
             engine.memset(tile_[:], 0.0)
             return tile_
 
@@ -85,6 +81,8 @@ def tile_list_twoownboards_storeleads_one_ownpage_kernel(
         pv = [board(nc.vector, "pv%d" % t, "pv%d" % t) for t in range(2)]
         wt_plane = zeroed_plane(V, "wt_plane")
         wb_plane = zeroed_plane(N, "wb_plane")
+        pv = pv + [board(nc.vector, "pv%d" % t, "pv%d" % t) for t in range(2, 4)]
+        pw = [board(nc.vector, "pw0", "pw0")]
 
         list1 = load_list(offs, "list1")
         wt_table = pool.tile([P, V], U32, name="wt_table", tag="wt_table", align_bytes=64)
@@ -156,17 +154,16 @@ def tile_list_twoownboards_storeleads_one_ownpage_kernel(
         w2_codes.append(reused.tile([P, 2 * P], I32, name="w2_codes1", offset=512, align_bytes=64))
         deal(w2_dealt[1], w2_plane, 2)
         deal(w2_codes[1], w2_raw, 2)
-        bank = psum.tile([P, 2, J], F32, name="b_bank2")
+        bank = whole_bank("b_bank2", 2, J, "b_first1")
         for t in range(2):
             for h in range(2):
                 product(bank[:, t, h * HALF : (h + 1) * HALF], w2_codes[1], w2_dealt[1], E5M2, t, h)
         b_rest = []
         for t in range(2):
-            rows = boards.tile([P, J], F32, name="b_rest%d" % t, offset=4096 * t + 1536, align_bytes=64)
+            rows = pool.tile([P, J], F32, name="b_rest%d" % t, align_bytes=64)
             nc.vector.tensor_copy(rows[:], bank[:, t, :])
             b_rest.append(rows)
 
-        pv = pv + [board(nc.gpsimd, "pv%d" % (t + 2), tag) for t, tag in enumerate(("b_lead1", "b_rows1"))]
         w_picked = pool.tile([P, R], U32, name="w_picked", align_bytes=64)
         w_picked_scales = reused.tile([P, R], U8, name="w_picked_scales", offset=512, align_bytes=64)
         nc.vector.tensor_copy(w_picked[:], wt_table[:].indirect(list1[:]))
@@ -201,7 +198,7 @@ def tile_list_twoownboards_storeleads_one_ownpage_kernel(
         fetch_b(0, 0)
         fetch_b(0, 1)
         scatter(pv[3], list4, 0, J, b_rest[1][:])
-        pw = [board(nc.gpsimd, "pw%d" % t, None, 2048 * t) for t in range(PACK)]
+        pw = pw + [board(nc.gpsimd, "pw%d" % (t + 1), tag) for t, tag in enumerate(("w_codes0", "w_codes1", "w_scales1"))]
         fetch_b(0, 2)
         for t in range(PACK):
             scatter(pw[t], list3, 0, J, a_rows[:, t, :])

from contextlib import ExitStack

import concourse.mybir as mybir

K, T, J, R, V, C, D, O, N, E = 512, 1024, 256, 512, 1024, 512, 512, 256, 256, 512
FLOPS = 2 * K * R * J * 2 + 2 * R * N * O

F32 = mybir.dt.float32
BF16 = mybir.dt.bfloat16
I32 = mybir.dt.int32
U32 = mybir.dt.uint32
U16 = mybir.dt.uint16
U8 = mybir.dt.uint8
E4M3 = mybir.dt.float8_e4m3fn_x4
E5M2 = mybir.dt.float8_e5m2_x4
E2M1 = mybir.dt.float4_e2m1fn_x4
COPY = mybir.ActivationFunctionType.Copy
ALU = mybir.AluOpType

P = 128
PACK = 4
HALF = 128
LANES = 16


def tile_list_twoownboards_storeleads_one_ownpage_kernel(
    tc, xt_words, xt_scales, wt_words, wt_scales, w2_words, w2_scales, sa, sb, wb_words, wb_scales,
    offs, offs2, offs3, offs4, offs5, offs6, offs7, out,
):
    nc = tc.nc

    with ExitStack() as ctx:
        lists = ctx.enter_context(tc.tile_pool(name="lists", bufs=1))
        pool = ctx.enter_context(tc.tile_pool(name="work", bufs=1))
        reused = ctx.enter_context(tc.tile_pool(name="reused", bufs=1))
        late = ctx.enter_context(tc.tile_pool(name="late", bufs=1))
        psum = ctx.enter_context(tc.psum_pool(name="psum", bufs=1))

        def load_list(src, name):
            dst = lists.tile([P, src.shape[1]], U16, name=name)
            nc.sync.dma_start(dst[:], src)
            return dst

        def entries(lst, first, count):
            return lst[:, first // LANES : (first + count) // LANES]

        def zeroed_plane(width, name):
            plane = pool.tile([P, width], U8, name=name, align_bytes=64)
            nc.vector.memset(plane[:].bitcast(I32), 0)
            return plane

        def load_scale_rows(queue, plane, scales, quadrants=range(4)):
            for q in quadrants:
                queue.dma_start(plane[32 * q : 32 * q + 4, :].bitcast(I32), scales[0, 4 * q : 4 * q + 4, :].bitcast(I32))

        def board(engine, name, tag):
            tile_ = pool.tile([P, C], F32, name=name, tag=tag, align_bytes=64)
            engine.memset(tile_[:], 0.0)
            return tile_

        def whole_bank(name, rows, width, tag=None):
            bank = psum.tile([P, 512], F32, name=name, tag=tag or name)
            return bank[:, 0 : rows * width].rearrange("p (r w) -> p r w", r=rows)

        w2_plane = zeroed_plane(2 * R, "w2_plane")
        xt_plane = reused.tile([P, T], U8, name="xt_plane", offset=0, align_bytes=64)
        nc.vector.memset(xt_plane[:].bitcast(I32), 0)
        list2 = load_list(offs2, "list2")
        xt_table = pool.tile([P, T], U16, name="xt_table", tag="xt_table", align_bytes=64)
        nc.sync.dma_start(xt_table[:].bitcast(I32), xt_words[0].bitcast(I32))
        w2_rows = w2_scales[0].bitcast(I32).rearrange("(u v r) c -> v r u c", u=2, v=2)
        w2_plane_words = w2_plane[:].bitcast(I32)
        for v in range(2):
            nc.sync.dma_start(w2_plane_words[32 * v : 32 * v + 4, :].rearrange("r (u c) -> r u c", u=2), w2_rows[v])
        load_scale_rows(nc.sync, xt_plane, xt_scales, range(0, 3))
        w2_raw = pool.tile([P, R], I32, name="w2_raw", tag="w2_raw", align_bytes=64)
        nc.sync.dma_start(w2_raw[:], w2_words[0].rearrange("p c r -> p (c r)").bitcast(I32))
        load_scale_rows(nc.sync, xt_plane, xt_scales, range(3, 4))
        list4 = load_list(offs4, "list4")

        pv = [board(nc.vector, "pv%d" % t, "pv%d" % t) for t in range(2)]
        wt_plane = zeroed_plane(V, "wt_plane")
        wb_plane = zeroed_plane(N, "wb_plane")
        pv = pv + [board(nc.vector, "pv%d" % t, "pv%d" % t) for t in range(2, 4)]
        pw = [board(nc.vector, "pw0", "pw0")]

        list1 = load_list(offs, "list1")
        wt_table = pool.tile([P, V], U32, name="wt_table", tag="wt_table", align_bytes=64)
        nc.sync.dma_start(wt_table[:].bitcast(I32), wt_words[0].rearrange("p c r -> p (c r)").bitcast(I32))
        load_scale_rows(nc.sync, wt_plane, wt_scales)
        list6 = load_list(offs6, "list6")
        sb_cols = pool.tile([P, PACK], F32, name="sb_cols")
        nc.sync.dma_start(sb_cols[:], sb.rearrange("(p t) o -> p (t o)", t=PACK))
        list3 = load_list(offs3, "list3")
        list5 = load_list(offs5, "list5")
        sa_cols = pool.tile([P, PACK], F32, name="sa_cols")
        nc.sync.dma_start(sa_cols[:], sa.rearrange("(p t) o -> p (t o)", t=PACK))
        wb_codes = pool.tile([P, 2 * N], U8, name="wb_codes", align_bytes=64)
        nc.sync.dma_start(wb_codes[:].bitcast(I32), wb_words[0].bitcast(I32))
        load_scale_rows(nc.sync, wb_plane, wb_scales)
        list7 = load_list(offs7, "list7")

        def deal(dst, src, t0):
            nc.vector.tensor_copy(
                dst[:].rearrange("p (t q) -> p t q", q=P),
                src[:, 0:R].rearrange("p (q t) -> p t q", t=PACK)[:, t0 : t0 + 2, :],
            )

        def product(bank, codes, scales, fmt, t, h):
            nc.tensor.matmul_mx(
                out=bank,
                lhsT=codes[:, t * P : (t + 1) * P].bitcast(fmt),
                lhsT_scale=scales[:, t * P : (t + 1) * P],
                rhs=x_codes[h][:].bitcast(E2M1),
                rhs_scale=x_scales[h][:],
                start=True,
                stop=True,
            )

        def scatter(window, lst, first, count, values):
            nc.scalar.activation(out=window[:].indirect(entries(lst, first, count)), in_=values, func=COPY)

        def fetch(dst, window, lst, first, count, scale):
            nc.scalar.activation(out=dst, in_=window[:].indirect(entries(lst, first, count)), func=COPY, scale=scale)

        x_codes = [pool.tile([P, HALF], U16, name="x_codes0", align_bytes=64)]
        x_scales = [pool.tile([P, HALF], U8, name="x_scales%d" % h, align_bytes=64) for h in range(2)]
        w2_codes = [pool.tile([P, 2 * P], I32, name="w2_codes0", align_bytes=64)]
        w2_dealt = [pool.tile([P, 2 * P], U8, name="w2_dealt0", align_bytes=64)]
        nc.vector.tensor_copy(x_codes[0][:], xt_table[:].indirect(entries(list2, 0, HALF)))
        nc.vector.tensor_copy(w2_plane_words[64:128, 0 : R // 4], w2_plane_words[0:64, R // 4 : R // 2])
        deal(w2_dealt[0], w2_plane, 0)
        deal(w2_codes[0], w2_raw, 0)
        for h in range(2):
            nc.vector.tensor_copy(x_scales[h][:], xt_plane[:].indirect(entries(list2, h * HALF, HALF)))
        x_codes.append(reused.tile([P, HALF], U16, name="x_codes1", offset=0, align_bytes=64))
        nc.vector.tensor_copy(x_codes[1][:], xt_table[:].indirect(entries(list2, HALF, HALF)))

        for t in range(2):
            bank = whole_bank("b_first%d" % t, 1, HALF)[:, 0, :]
            product(bank, w2_codes[0], w2_dealt[0], E5M2, t, 0)
            rows = pool.tile([P, HALF], F32, name="b_lead%d" % t, align_bytes=64)
            nc.scalar.activation(out=rows[:], in_=bank, func=COPY)
            scatter(pv[t], list4, 0, HALF, rows[:])
        bank = whole_bank("b_bank1", 2, HALF)
        for t in range(2):
            product(bank[:, t, :], w2_codes[0], w2_dealt[0], E5M2, t, 1)
        rows = pool.tile([P, 2, HALF], F32, name="b_rows1", align_bytes=64)
        nc.vector.tensor_copy(rows[:], bank)
        for t in range(2):
            scatter(pv[t], list4, HALF, HALF, rows[:, t, :])

        w2_dealt.append(reused.tile([P, 2 * P], U8, name="w2_dealt1", offset=256, align_bytes=64))
        w2_codes.append(reused.tile([P, 2 * P], I32, name="w2_codes1", offset=512, align_bytes=64))
        deal(w2_dealt[1], w2_plane, 2)
        deal(w2_codes[1], w2_raw, 2)
        bank = whole_bank("b_bank2", 2, J, "b_first1")
        for t in range(2):
            for h in range(2):
                product(bank[:, t, h * HALF : (h + 1) * HALF], w2_codes[1], w2_dealt[1], E5M2, t, h)
        b_rest = []
        for t in range(2):
            rows = pool.tile([P, J], F32, name="b_rest%d" % t, align_bytes=64)
            nc.vector.tensor_copy(rows[:], bank[:, t, :])
            b_rest.append(rows)

        w_picked = pool.tile([P, R], U32, name="w_picked", align_bytes=64)
        w_picked_scales = reused.tile([P, R], U8, name="w_picked_scales", offset=512, align_bytes=64)
        nc.vector.tensor_copy(w_picked[:], wt_table[:].indirect(list1[:]))
        nc.vector.tensor_copy(w_picked_scales[:], wt_plane[:].indirect(list1[:]))
        a_rows = late.tile([P, PACK, J], F32, name="a_rows", offset=0, align_bytes=64)
        for u in range(2):
            w_codes = pool.tile([P, 2 * P], U32, name="w_codes%d" % u, align_bytes=64)
            w_scales = pool.tile([P, 2 * P], U8, name="w_scales%d" % u, align_bytes=64)
            deal(w_codes, w_picked, 2 * u)
            deal(w_scales, w_picked_scales, 2 * u)
            bank = psum.tile([P, 2, J], F32, name="a_bank%d" % u)
            for t in range(2):
                for h in range(2):
                    product(bank[:, t, h * HALF : (h + 1) * HALF], w_codes, w_scales, E4M3, t, h)
            nc.vector.tensor_copy(a_rows[:, 2 * u : 2 * u + 2, :], bank[:])

        picked = [pool.tile([P, 2, PACK, HALF], F32, name="picked0", align_bytes=64)]
        diff = [pool.tile([P, PACK, HALF], F32, name="diff%d" % h, align_bytes=64) for h in range(2)]

        def fetch_a(h, t, lo=0, hi=HALF):
            fetch(picked[h][:, 0, t, lo:hi], pw[t], list5, h * HALF + lo, hi - lo, sa_cols[:, t : t + 1])

        def fetch_b(h, t, lo=0, hi=HALF):
            fetch(picked[h][:, 1, t, lo:hi], pv[t], list6, h * HALF + lo, hi - lo, sb_cols[:, t : t + 1])

        def subtract(h, t, lo=0, hi=HALF):
            nc.vector.tensor_tensor(
                diff[h][:, t, lo:hi], picked[h][:, 0, t, lo:hi], picked[h][:, 1, t, lo:hi], ALU.subtract
            )

        scatter(pv[2], list4, 0, J, b_rest[0][:])
        fetch_b(0, 0)
        fetch_b(0, 1)
        scatter(pv[3], list4, 0, J, b_rest[1][:])
        pw = pw + [board(nc.gpsimd, "pw%d" % (t + 1), tag) for t, tag in enumerate(("w_codes0", "w_codes1", "w_scales1"))]
        fetch_b(0, 2)
        for t in range(PACK):
            scatter(pw[t], list3, 0, J, a_rows[:, t, :])
            if t == 0:
                fetch_b(0, 3)
            else:
                fetch_a(0, t - 1)
                subtract(0, t - 1)
        for lo in (0, HALF // 2):
            fetch_a(0, PACK - 1, lo, lo + HALF // 2)
            subtract(0, PACK - 1, lo, lo + HALF // 2)

        page = [board(nc.gpsimd, "page%d" % m, tag) for m, tag in enumerate(("x_codes0", "x_scales0"))]

        hid = [pool.tile([P, HALF * PACK], BF16, name="hid%d" % h, align_bytes=64) for h in range(2)]
        hid_codes = [pool.tile([P, HALF], U32, name="hid_codes%d" % h, align_bytes=64) for h in range(2)]
        hid_scales = [pool.tile([P, HALF], U8, name="hid_scales%d" % h, align_bytes=64) for h in range(2)]

        def quantise(h, lo=0, hi=HALF):
            values = hid[h][:, lo * PACK : hi * PACK]
            woven = diff[h][:, :, lo:hi].rearrange("p t o -> p o t")
            nc.vector.scalar_tensor_tensor(
                values.rearrange("p (o t) -> p o t", t=PACK), woven, -1.0, woven, ALU.mult, ALU.max
            )
            nc.vector.quantize_mx(out=hid_codes[h][:, lo:hi].bitcast(E5M2), scales=hid_scales[h][:, lo:hi], in_=values)

        def output_product(bank, h, m):
            nc.tensor.matmul_mx(
                out=bank,
                lhsT=wb_codes[:, 2 * m * P : 2 * (m + 1) * P].bitcast(E2M1),
                lhsT_scale=wb_plane[:, m * P : (m + 1) * P],
                rhs=hid_codes[h][:].bitcast(E5M2),
                rhs_scale=hid_scales[h][:],
                start=True,
                stop=True,
            )

        for lo in (0, HALF // 2):
            quantise(0, lo, lo + HALF // 2)
        banks = [whole_bank("p_bank0%d" % m, 1, HALF, ("b_first0", "a_bank0")[m])[:, 0, :] for m in range(2)]
        for m in range(2):
            output_product(banks[m], 0, m)
        picked.append(late.tile([P, 2, PACK, HALF], F32, name="picked1", offset=0, align_bytes=64))
        for t in range(PACK - 1):
            fetch_a(1, t)
            fetch_b(1, t)
            subtract(1, t)
        for lo in (0, HALF // 2):
            fetch_a(1, PACK - 1, lo, lo + HALF // 2)
            fetch_b(1, PACK - 1, lo, lo + HALF // 2)
            subtract(1, PACK - 1, lo, lo + HALF // 2)
            quantise(1, lo, lo + HALF // 2)
        for m in range(2):
            rows = pool.tile([P, HALF], F32, name="p_rows0%d" % m, align_bytes=64)
            if m == 0:
                nc.scalar.activation(out=rows[:], in_=banks[m], func=COPY)
            else:
                nc.vector.tensor_copy(rows[:], banks[m])
            scatter(page[m], list7, 0, HALF, rows[:])
        for m in range(2):
            bank = whole_bank("p_bank1%d" % m, 1, HALF, ("b_first1", "b_bank1")[m])[:, 0, :]
            output_product(bank, 1, m)
            rows = pool.tile([P, HALF], F32, name="p_rows1%d" % m, align_bytes=64)
            nc.vector.tensor_copy(rows[:], bank)
            scatter(page[m], list7, HALF, HALF, rows[:])
            nc.sync.dma_start(out[m * P : (m + 1) * P, :], page[m][:])
